import numpy as np
import ml_dtypes


def mxq(x, axis, fmt="e4m3"):
    dtype, down = {"e4m3": (ml_dtypes.float8_e4m3fn, 7), "e5m2": (ml_dtypes.float8_e5m2, 14)}[fmt]
    v = np.moveaxis(np.asarray(x, np.float32).astype(ml_dtypes.bfloat16).astype(np.float64), axis, -1)
    blocks = v.reshape(v.shape[:-1] + (-1, 32))
    amax = np.abs(blocks).max(-1, keepdims=True)
    byte = np.maximum(np.where(amax > 0, np.frexp(amax)[1] - 1 + 127, 0) - down, 1)
    scale = np.exp2(byte - 127.0)
    codes = (blocks / scale).astype(np.float32).astype(dtype).astype(np.float64)
    return np.moveaxis((codes * scale).reshape(v.shape), -1, axis)


WIDE = False


def mx_kscale(k):
    if not WIDE:
        return np.ones(k)
    levels = np.array([10, -10, 5, -5, 0])
    if k % 512:
        return np.exp2(np.random.permutation(np.resize(levels, k // 32))).repeat(32)
    a = np.empty((k // 512, 16))
    for p in range(k // 512):
        a[p, :8] = np.random.permutation(np.resize(levels, 8))
        for g in range(8):
            far = levels[np.abs(levels - a[p, g]) >= 10]
            a[p, g + 8] = far[np.random.randint(len(far))]
    return np.exp2(a.ravel()).repeat(32)


def f64(x):
    return np.asarray(x).astype(np.float64)


def striped(idx):
    return np.tile(idx.reshape(-1, 16).T, (8, 1)).astype(np.uint16)


def unstriped(offs):
    return offs[:16].T.reshape(-1).astype(np.int64)


def relu(v):
    return np.maximum(v, 0.0)


K, T, E, C, H, N = 1024, 768, 6, 256, 512, 128


def by_expert(wq, xq):
    return np.concatenate([wq[e].T @ xq[:, e * C:(e + 1) * C] for e in range(E)], axis=1)


def setup_inputs():
    n = np.random.standard_normal
    s = mx_kscale(K)[:, None]
    u = mx_kscale(H)
    first = np.random.permutation(np.repeat(np.arange(E), T // E))
    second = (first + 1 + np.random.permutation(np.repeat(np.arange(E - 1), -(-T // (E - 1)))[:T])) % E
    while np.bincount(second, minlength=E).max() != T // E:
        load = np.bincount(second, minlength=E); hi, lo = int(load.argmax()), int(load.argmin())
        t = np.flatnonzero((second == hi) & (first != lo))[0]; second[t] = lo
    slot_token = np.empty(E * C, np.int64); pos = np.empty((2, T), np.int64); fill = np.zeros(E, np.int64)
    place = np.stack([np.random.permutation(C) for _ in range(E)])
    for r, deal in enumerate((first, second)):
        for t in np.random.permutation(T):
            e = deal[t]; j = e * C + place[e, fill[e]]; fill[e] += 1; slot_token[j] = t; pos[r, t] = j
    g = np.random.uniform(0.2, 0.8, T)
    return {
        "xT": (n((K, T)) * s).astype(np.float32),
        "w1": (n((E, K, H)) / np.sqrt(K) / s[None]).astype(np.float32),
        "w3": (n((E, K, H)) / np.sqrt(K) / s[None] * u[None, None, :]).astype(np.float32),
        "w2": (n((E, H, N)) / np.sqrt(H) / u[None, :, None]).astype(np.float32),
        "gate": np.stack([np.tile(g, (N, 1)), np.tile(1.0 - g, (N, 1))]).astype(np.float32),
        "offs": striped(slot_token),
        "pos1": striped(pos[0]),
        "pos2": striped(pos[1]),
    }


def reference(xT, w1, w3, w2, gate, offs, pos1, pos2):
    idx = unstriped(offs)
    xq = mxq(f64(xT)[:, idx], 0, "e4m3")
    h = relu(by_expert(mxq(f64(w1), 1, "e4m3"), xq))
    h = h * by_expert(mxq(f64(w3), 1, "e4m3"), xq)
    y = by_expert(mxq(f64(w2), 1, "e4m3"), mxq(h, 0, "e4m3"))
    return f64(gate[0]) * y[:, unstriped(pos1)] + f64(gate[1]) * y[:, unstriped(pos2)]

@@ -1,0 +1,266 @@
+from contextlib import ExitStack
+
+import concourse.mybir as mybir
+
+K, T, E, C, H, N = 1024, 768, 6, 256, 512, 128
+P = 128
+PACK = 4
+K_PASS = P * PACK
+PASSES = K // K_PASS
+SLOTS = E * C
+FLOPS = 2 * SLOTS * (2 * K * H + H * N)
+
+F32 = mybir.dt.float32
+BF16 = mybir.dt.bfloat16
+U32 = mybir.dt.uint32
+U16 = mybir.dt.uint16
+U8 = mybir.dt.uint8
+FP8X4 = mybir.dt.float8_e4m3fn_x4
+MULT = mybir.AluOpType.mult
+ADD = mybir.AluOpType.add
+RELU = mybir.ActivationFunctionType.Relu
+
+SLICE = 512
+HALF = 128
+PIECE = 256
+AHEAD = 9
+SHARE = 88
+LAST_SHARE = 48
+SCALE_ROW = (0, 4)
+
+
+def tile_routed_moe_kernel(tc, xT, w1, w3, w2, gate, offs, pos1, pos2, out):
+    nc = tc.nc
+    with ExitStack() as ctx:
+        keep = ctx.enter_context(tc.tile_pool(name="keep", bufs=1))
+        stage = ctx.enter_context(tc.tile_pool(name="stage", bufs=11))
+        work = ctx.enter_context(tc.tile_pool(name="work", bufs=3))
+        quant = ctx.enter_context(tc.tile_pool(name="quant", bufs=10))
+        psum = ctx.enter_context(tc.psum_pool(name="psum", bufs=3))
+        psum_y = ctx.enter_context(tc.psum_pool(name="psum_y", bufs=2))
+
+        offs_t = keep.tile([P, SLOTS // 16], U16, name="offs_t")
+        pos1_t = keep.tile([P, T // 16], U16, name="pos1_t")
+        pos2_t = keep.tile([P, T // 16], U16, name="pos2_t")
+        x_raw = [keep.tile([P, PACK, T], F32, name=f"x_raw{s}") for s in range(PASSES)]
+        x_bf = [keep.tile([P, T * PACK], BF16, name=f"x_bf{s}", align_bytes=64) for s in range(PASSES)]
+        x_words = [keep.tile([P, T], U32, name=f"x_words{s}", align_bytes=64) for s in range(PASSES)]
+        x_bytes = keep.tile([P, T], U8, name="x_bytes", align_bytes=64)
+        slot_words = {}
+        slot_bytes = {}
+        y_all = keep.tile([P, SLOTS], F32, name="y_all")
+
+        nc.gpsimd.memset(x_bytes[:], 0)
+        nc.sync.dma_start(offs_t[:], offs)
+        for s in range(PASSES):
+            nc.sync.dma_start(
+                out=x_raw[s][:], in_=xT[s * K_PASS : (s + 1) * K_PASS, :].rearrange("(p t) n -> p t n", t=PACK)
+            )
+
+        tiles = [(w, e, s) for e in range(E) for w in (0, 1) for s in range(PASSES)]
+        raws = {}
+        cast = {}
+        quantised = {}
+        w2_raw = {}
+        w2_cast = {}
+        w2_quantised = {}
+        relus = {}
+        sums = {}
+        hidden = {}
+        hidden_q = {}
+        results = {}
+
+        def load(i):
+            w, e, s = tiles[i]
+            raw = stage.tile([P, PACK, H], F32, name="raw")
+            nc.sync.dma_start(
+                out=raw[:],
+                in_=(w1, w3)[w][e, s * K_PASS : (s + 1) * K_PASS, :].rearrange("(p t) c -> p t c", t=PACK),
+            )
+            raws[i] = raw
+
+        def load_w2(e):
+            raw = stage.tile([P, PACK, N], F32, name="raw")
+            nc.sync.dma_start(out=raw[:], in_=w2[e].rearrange("(p t) n -> p t n", t=PACK))
+            w2_raw[e] = raw
+
+        def cast_w(i, scalar_m):
+            w_bf = work.tile([P, H * PACK], BF16, name="w_bf", align_bytes=64, bufs=4)
+            dst = w_bf[:].rearrange("p (t m k) -> p m k t", t=PACK, k=PACK)
+            src = raws[i][:].rearrange("p k (m t) -> p m k t", t=PACK)
+            nc.scalar.copy(dst[:, 0:scalar_m], src[:, 0:scalar_m])
+            if scalar_m < P:
+                nc.vector.tensor_copy(dst[:, scalar_m:P], src[:, scalar_m:P])
+            cast[i] = w_bf
+
+        def quantise_w(i):
+            words = quant.tile([P, H], U32, name="w_words", align_bytes=64)
+            scales = quant.tile([P, H], U8, name="w_scales", align_bytes=64)
+            nc.vector.quantize_mx(out=words[:].bitcast(FP8X4), scales=scales[:], in_=cast[i][:])
+            quantised[tiles[i]] = (words, scales)
+
+        def cast_w2(e):
+            w_bf = work.tile([P, N * PACK], BF16, name="w2_bf", align_bytes=64, bufs=2)
+            nc.vector.tensor_copy(
+                w_bf[:].rearrange("p (c i t) -> p c t i", i=4, t=PACK),
+                w2_raw[e][:].rearrange("p t (c i) -> p c t i", i=4),
+            )
+            w2_cast[e] = w_bf
+
+        def quantise_w2(e):
+            words = work.tile([P, N], U32, name="w2_words", align_bytes=64)
+            scales = work.tile([P, N], U8, name="w2_scales", align_bytes=64)
+            nc.vector.quantize_mx(out=words[:].bitcast(FP8X4), scales=scales[:], in_=w2_cast[e][:])
+            w2_quantised[e] = (words, scales)
+
+        def gather_words(q, s):
+            a, b = q * SLICE, (q + 1) * SLICE
+            if s == 0:
+                words = work.tile([P, PASSES, SLICE], U32, name="slot_words", align_bytes=64, bufs=2)
+                slot_words[q] = words
+            nc.vector.tensor_copy(slot_words[q][:, s, :], x_words[s][:].indirect(offs_t[:, a // 16 : b // 16]))
+
+        def gather_bytes(q):
+            a, b = q * SLICE, (q + 1) * SLICE
+            scales = work.tile([P, SLICE], U8, name="slot_bytes", align_bytes=64, bufs=2)
+            nc.vector.tensor_copy(scales[:], x_bytes[:].indirect(offs_t[:, a // 16 : b // 16]))
+            slot_bytes[q] = scales
+
+        def project(w, e, half):
+            q, a = divmod(e * C + half * HALF, SLICE)
+            acc = psum.tile([P, PACK, HALF], F32, name=("acc_a", "acc_b")[w])
+            for t in range(PACK):
+                for s in range(PASSES):
+                    words, scales = quantised[(w, e, s)]
+                    nc.tensor.matmul_mx(
+                        out=acc[:, t, :],
+                        lhsT=words[:, t * P : (t + 1) * P].bitcast(FP8X4),
+                        lhsT_scale=scales[:, t * P : (t + 1) * P],
+                        rhs=slot_words[q][:, s, a : a + HALF].bitcast(FP8X4),
+                        rhs_scale=slot_bytes[q][SCALE_ROW[s] : P, a : a + HALF],
+                        start=(s == 0),
+                        stop=(s == PASSES - 1),
+                    )
+            sums[(w, e, half)] = acc
+
+        def rectify(e, half):
+            r = raws[4 * e + 3][:, :, half * HALF : (half + 1) * HALF].rearrange("p k (n t) -> p k n t", t=PACK)
+            nc.scalar.activation(r, sums[(0, e, half)][:].rearrange("p t (k n) -> p k n t", k=PACK), RELU)
+            relus[(e, half)] = r
+
+        def hide(e, half):
+            h = work.tile([P, HALF, PACK], BF16, name="h", align_bytes=64)
+            nc.vector.tensor_tensor(
+                h[:].rearrange("p (k n) t -> p k n t", k=PACK),
+                sums[(1, e, half)][:].rearrange("p t (k n) -> p k n t", k=PACK),
+                relus[(e, half)],
+                MULT,
+            )
+            hidden[(e, half)] = h
+
+        def quantise_h(e, half):
+            words = work.tile([P, HALF], U32, name="h_words", align_bytes=64)
+            scales = work.tile([P, HALF], U8, name="h_scales", align_bytes=64)
+            nc.vector.quantize_mx(
+                out=words[:].bitcast(FP8X4),
+                scales=scales[:],
+                in_=hidden[(e, half)][:].rearrange("p n t -> p (n t)"),
+            )
+            hidden_q[(e, half)] = (words, scales)
+
+        def project_back(e, half):
+            acc = psum_y.tile([P, HALF], F32, name="acc_y")
+            w_words, w_scales = w2_quantised[e]
+            h_words, h_scales = hidden_q[(e, half)]
+            nc.tensor.matmul_mx(
+                out=acc[:],
+                lhsT=w_words[:].bitcast(FP8X4),
+                lhsT_scale=w_scales[:],
+                rhs=h_words[:].bitcast(FP8X4),
+                rhs_scale=h_scales[:],
+                start=True,
+                stop=True,
+            )
+            results[(e, half)] = acc
+
+        def keep_y(e, half):
+            a = e * C + half * HALF
+            nc.vector.tensor_copy(y_all[:, a : a + HALF], results[(e, half)][:])
+
+        def load_next(i):
+            if i < len(tiles):
+                load(i)
+                if i % 4 == 3:
+                    load_w2(i // 4)
+
+        for i in range(AHEAD):
+            load_next(i)
+        for s in range(PASSES):
+            dst = x_bf[s][:].rearrange("p (c i t) -> p c t i", i=4, t=PACK)
+            src = x_raw[s][:].rearrange("p t (c i) -> p c t i", i=4)
+            nc.scalar.copy(dst[:, 128:192], src[:, 128:192])
+            nc.vector.tensor_copy(dst[:, 0:128], src[:, 0:128])
+            for a, b in ((0, 512), (512, 768)):
+                nc.vector.quantize_mx(
+                    out=x_words[s][:, a:b].bitcast(FP8X4),
+                    scales=x_bytes[SCALE_ROW[s] : P, a:b],
+                    in_=x_bf[s][:, PACK * a : PACK * b],
+                )
+            gather_words(0, s)
+        gather_bytes(0)
+        nc.sync.dma_start(pos1_t[:], pos1)
+        nc.sync.dma_start(pos2_t[:], pos2)
+
+        gate_t = None
+        last = len(tiles) - 1
+        for i in range(len(tiles) + 4):
+            e, r = divmod(i, 4)
+            load_next(i + AHEAD)
+            if i + AHEAD == last:
+                gate_t = stage.tile([P, 2, T], F32, name="raw")
+                nc.sync.dma_start(out=gate_t[:], in_=gate.rearrange("r p t -> p r t"))
+            if i <= last:
+                cast_w(i, LAST_SHARE if i == last else SHARE)
+            if 1 <= i <= last + 1:
+                quantise_w(i - 1)
+            if r == 2 and e < E:
+                for half in range(2):
+                    project(0, e, half)
+            if r == 3 and e < E:
+                cast_w2(e)
+                for half in range(2):
+                    rectify(e, half)
+            if r == 0 and e > 0:
+                for half in range(2):
+                    project(1, e - 1, half)
+                quantise_w2(e - 1)
+            if r == 1 and e > 0:
+                for half in range(2):
+                    hide(e - 1, half)
+            if r == 2 and e > 0:
+                for half in range(2):
+                    quantise_h(e - 1, half)
+                for half in range(2):
+                    project_back(e - 1, half)
+            if r == 3 and e > 0:
+                for half in range(2):
+                    keep_y(e - 1, half)
+            if i in (6, 7):
+                gather_words(1, i - 6)
+            if i == 8:
+                gather_bytes(1)
+            if i in (12, 13):
+                gather_words(2, i - 12)
+            if i == 14:
+                gather_bytes(2)
+
+        for c in range(T // PIECE):
+            a, b = c * PIECE, (c + 1) * PIECE
+            idx = slice(a // 16, b // 16)
+            u = work.tile([P, PIECE], F32, name="u")
+            v = work.tile([P, PIECE], F32, name="v")
+            o = work.tile([P, PIECE], F32, name="o")
+            nc.vector.tensor_tensor(u[:], y_all[:].indirect(pos1_t[:, idx]), gate_t[:, 0, a:b], MULT)
+            nc.vector.tensor_tensor(v[:], y_all[:].indirect(pos2_t[:, idx]), gate_t[:, 1, a:b], MULT)
+            nc.vector.tensor_tensor(o[:], u[:], v[:], ADD)
+            nc.sync.dma_start(out=out[:, a:b], in_=o[:])

@@ -24,8 +24,8 @@ SLICE = 512
 HALF = 128
 PIECE = 256
 AHEAD = 9
-SHARE = 88
-LAST_SHARE = 48
+SHARE = 80
+LAST_SHARE = 44
 SCALE_ROW = (0, 4)
 
 
@@ -58,6 +58,7 @@ def tile_routed_moe_kernel(tc, xT, w1, w3, w2, gate, offs, pos1, pos2, out):
             )
 
         tiles = [(w, e, s) for e in range(E) for w in (0, 1) for s in range(PASSES)]
+        last = len(tiles) - 1
         raws = {}
         cast = {}
         quantised = {}
@@ -96,12 +97,18 @@ def tile_routed_moe_kernel(tc, xT, w1, w3, w2, gate, offs, pos1, pos2, out):
         def quantise_w(i):
             words = quant.tile([P, H], U32, name="w_words", align_bytes=64)
             scales = quant.tile([P, H], U8, name="w_scales", align_bytes=64)
-            nc.vector.quantize_mx(out=words[:].bitcast(FP8X4), scales=scales[:], in_=cast[i][:])
+            step = H // 2 if i == last else H
+            for a in range(0, H, step):
+                nc.vector.quantize_mx(
+                    out=words[:, a : a + step].bitcast(FP8X4),
+                    scales=scales[:, a : a + step],
+                    in_=cast[i][:, PACK * a : PACK * (a + step)],
+                )
             quantised[tiles[i]] = (words, scales)
 
         def cast_w2(e):
             w_bf = work.tile([P, N * PACK], BF16, name="w2_bf", align_bytes=64, bufs=2)
-            nc.vector.tensor_copy(
+            nc.scalar.copy(
                 w_bf[:].rearrange("p (c i t) -> p c t i", i=4, t=PACK),
                 w2_raw[e][:].rearrange("p t (c i) -> p c t i", i=4),
             )
@@ -212,7 +219,6 @@ def tile_routed_moe_kernel(tc, xT, w1, w3, w2, gate, offs, pos1, pos2, out):
         nc.sync.dma_start(pos2_t[:], pos2)
 
         gate_t = None
-        last = len(tiles) - 1
         for i in range(len(tiles) + 4):
             e, r = divmod(i, 4)
             load_next(i + AHEAD)
@@ -254,13 +260,26 @@ def tile_routed_moe_kernel(tc, xT, w1, w3, w2, gate, offs, pos1, pos2, out):
             if i == 14:
                 gather_bytes(2)
 
-        for c in range(T // PIECE):
-            a, b = c * PIECE, (c + 1) * PIECE
-            idx = slice(a // 16, b // 16)
-            u = work.tile([P, PIECE], F32, name="u")
-            v = work.tile([P, PIECE], F32, name="v")
-            o = work.tile([P, PIECE], F32, name="o")
-            nc.vector.tensor_tensor(u[:], y_all[:].indirect(pos1_t[:, idx]), gate_t[:, 0, a:b], MULT)
-            nc.vector.tensor_tensor(v[:], y_all[:].indirect(pos2_t[:, idx]), gate_t[:, 1, a:b], MULT)
-            nc.vector.tensor_tensor(o[:], u[:], v[:], ADD)
+        pieces = ((0, 512), (512, T))
+        products = {}
+
+        def fetch(piece, which, pos_t):
+            a, b = piece
+            prod = work.tile([P, b - a], F32, name=f"prod{which}", bufs=2)
+            nc.vector.tensor_tensor(
+                prod[:], y_all[:].indirect(pos_t[:, a // 16 : b // 16]), gate_t[:, which, a:b], MULT
+            )
+            products[(piece, which)] = prod
+
+        def finish(piece):
+            a, b = piece
+            o = work.tile([P, b - a], F32, name="o", bufs=2)
+            nc.vector.tensor_tensor(o[:], products[(piece, 0)][:], products[(piece, 1)][:], ADD)
             nc.sync.dma_start(out=out[:, a:b], in_=o[:])
+
+        fetch(pieces[0], 0, pos1_t)
+        fetch(pieces[0], 1, pos2_t)
+        fetch(pieces[1], 0, pos1_t)
+        finish(pieces[0])
+        fetch(pieces[1], 1, pos2_t)
+        finish(pieces[1])

@@ -24,7 +24,7 @@ SLICE = 512
 HALF = 128
 PIECE = 256
 AHEAD = 9
-SHARE = 80
+SHARE = 88
 LAST_SHARE = 44
 SCALE_ROW = (0, 4)
 
@@ -192,7 +192,8 @@ def tile_routed_moe_kernel(tc, xT, w1, w3, w2, gate, offs, pos1, pos2, out):
 
         def keep_y(e, half):
             a = e * C + half * HALF
-            nc.vector.tensor_copy(y_all[:, a : a + HALF], results[(e, half)][:])
+            copy = nc.scalar.copy if e == E - 1 else nc.vector.tensor_copy
+            copy(y_all[:, a : a + HALF], results[(e, half)][:])
 
         def load_next(i):
             if i < len(tiles):
@@ -280,6 +281,6 @@ def tile_routed_moe_kernel(tc, xT, w1, w3, w2, gate, offs, pos1, pos2, out):
         fetch(pieces[0], 0, pos1_t)
         fetch(pieces[0], 1, pos2_t)
         fetch(pieces[1], 0, pos1_t)
-        finish(pieces[0])
         fetch(pieces[1], 1, pos2_t)
+        finish(pieces[0])
         finish(pieces[1])

from contextlib import ExitStack

import concourse.mybir as mybir

K, T, E, C, H, N = 1024, 768, 6, 256, 512, 128
P = 128
PACK = 4
K_PASS = P * PACK
PASSES = K // K_PASS
SLOTS = E * C
FLOPS = 2 * SLOTS * (2 * K * H + H * N)

F32 = mybir.dt.float32
BF16 = mybir.dt.bfloat16
U32 = mybir.dt.uint32
U16 = mybir.dt.uint16
U8 = mybir.dt.uint8
FP8X4 = mybir.dt.float8_e4m3fn_x4
MULT = mybir.AluOpType.mult
ADD = mybir.AluOpType.add
RELU = mybir.ActivationFunctionType.Relu

SLICE = 512
HALF = 128
PIECE = 256
AHEAD = 9
SHARE = 88
LAST_SHARE = 44
SCALE_ROW = (0, 4)


def tile_routed_moe_kernel(tc, xT, w1, w3, w2, gate, offs, pos1, pos2, out):
    nc = tc.nc
    with ExitStack() as ctx:
        keep = ctx.enter_context(tc.tile_pool(name="keep", bufs=1))
        stage = ctx.enter_context(tc.tile_pool(name="stage", bufs=11))
        work = ctx.enter_context(tc.tile_pool(name="work", bufs=3))
        quant = ctx.enter_context(tc.tile_pool(name="quant", bufs=10))
        psum = ctx.enter_context(tc.psum_pool(name="psum", bufs=3))
        psum_y = ctx.enter_context(tc.psum_pool(name="psum_y", bufs=2))

        offs_t = keep.tile([P, SLOTS // 16], U16, name="offs_t")
        pos1_t = keep.tile([P, T // 16], U16, name="pos1_t")
        pos2_t = keep.tile([P, T // 16], U16, name="pos2_t")
        x_raw = [keep.tile([P, PACK, T], F32, name=f"x_raw{s}") for s in range(PASSES)]
        x_bf = [keep.tile([P, T * PACK], BF16, name=f"x_bf{s}", align_bytes=64) for s in range(PASSES)]
        x_words = [keep.tile([P, T], U32, name=f"x_words{s}", align_bytes=64) for s in range(PASSES)]
        x_bytes = keep.tile([P, T], U8, name="x_bytes", align_bytes=64)
        slot_words = {}
        slot_bytes = {}
        y_all = keep.tile([P, SLOTS], F32, name="y_all")

        nc.gpsimd.memset(x_bytes[:], 0)
        nc.sync.dma_start(offs_t[:], offs)
        for s in range(PASSES):
            nc.sync.dma_start(
                out=x_raw[s][:], in_=xT[s * K_PASS : (s + 1) * K_PASS, :].rearrange("(p t) n -> p t n", t=PACK)
            )

        tiles = [(w, e, s) for e in range(E) for w in (0, 1) for s in range(PASSES)]
        last = len(tiles) - 1
        raws = {}
        cast = {}
        quantised = {}
        w2_raw = {}
        w2_cast = {}
        w2_quantised = {}
        relus = {}
        sums = {}
        hidden = {}
        hidden_q = {}
        results = {}

        def load(i):
            w, e, s = tiles[i]
            raw = stage.tile([P, PACK, H], F32, name="raw")
            nc.sync.dma_start(
                out=raw[:],
                in_=(w1, w3)[w][e, s * K_PASS : (s + 1) * K_PASS, :].rearrange("(p t) c -> p t c", t=PACK),
            )
            raws[i] = raw

        def load_w2(e):
            raw = stage.tile([P, PACK, N], F32, name="raw")
            nc.sync.dma_start(out=raw[:], in_=w2[e].rearrange("(p t) n -> p t n", t=PACK))
            w2_raw[e] = raw

        def cast_w(i, scalar_m):
            w_bf = work.tile([P, H * PACK], BF16, name="w_bf", align_bytes=64, bufs=4)
            dst = w_bf[:].rearrange("p (t m k) -> p m k t", t=PACK, k=PACK)
            src = raws[i][:].rearrange("p k (m t) -> p m k t", t=PACK)
            nc.scalar.copy(dst[:, 0:scalar_m], src[:, 0:scalar_m])
            if scalar_m < P:
                nc.vector.tensor_copy(dst[:, scalar_m:P], src[:, scalar_m:P])
            cast[i] = w_bf

        def quantise_w(i):
            words = quant.tile([P, H], U32, name="w_words", align_bytes=64)
            scales = quant.tile([P, H], U8, name="w_scales", align_bytes=64)
            step = H // 2 if i == last else H
            for a in range(0, H, step):
                nc.vector.quantize_mx(
                    out=words[:, a : a + step].bitcast(FP8X4),
                    scales=scales[:, a : a + step],
                    in_=cast[i][:, PACK * a : PACK * (a + step)],
                )
            quantised[tiles[i]] = (words, scales)

        def cast_w2(e):
            w_bf = work.tile([P, N * PACK], BF16, name="w2_bf", align_bytes=64, bufs=2)
            nc.scalar.copy(
                w_bf[:].rearrange("p (c i t) -> p c t i", i=4, t=PACK),
                w2_raw[e][:].rearrange("p t (c i) -> p c t i", i=4),
            )
            w2_cast[e] = w_bf

        def quantise_w2(e):
            words = work.tile([P, N], U32, name="w2_words", align_bytes=64)
            scales = work.tile([P, N], U8, name="w2_scales", align_bytes=64)
            nc.vector.quantize_mx(out=words[:].bitcast(FP8X4), scales=scales[:], in_=w2_cast[e][:])
            w2_quantised[e] = (words, scales)

        def gather_words(q, s):
            a, b = q * SLICE, (q + 1) * SLICE
            if s == 0:
                words = work.tile([P, PASSES, SLICE], U32, name="slot_words", align_bytes=64, bufs=2)
                slot_words[q] = words
            nc.vector.tensor_copy(slot_words[q][:, s, :], x_words[s][:].indirect(offs_t[:, a // 16 : b // 16]))

        def gather_bytes(q):
            a, b = q * SLICE, (q + 1) * SLICE
            scales = work.tile([P, SLICE], U8, name="slot_bytes", align_bytes=64, bufs=2)
            nc.vector.tensor_copy(scales[:], x_bytes[:].indirect(offs_t[:, a // 16 : b // 16]))
            slot_bytes[q] = scales

        def project(w, e, half):
            q, a = divmod(e * C + half * HALF, SLICE)
            acc = psum.tile([P, PACK, HALF], F32, name=("acc_a", "acc_b")[w])
            for t in range(PACK):
                for s in range(PASSES):
                    words, scales = quantised[(w, e, s)]
                    nc.tensor.matmul_mx(
                        out=acc[:, t, :],
                        lhsT=words[:, t * P : (t + 1) * P].bitcast(FP8X4),
                        lhsT_scale=scales[:, t * P : (t + 1) * P],
                        rhs=slot_words[q][:, s, a : a + HALF].bitcast(FP8X4),
                        rhs_scale=slot_bytes[q][SCALE_ROW[s] : P, a : a + HALF],
                        start=(s == 0),
                        stop=(s == PASSES - 1),
                    )
            sums[(w, e, half)] = acc

        def rectify(e, half):
            r = raws[4 * e + 3][:, :, half * HALF : (half + 1) * HALF].rearrange("p k (n t) -> p k n t", t=PACK)
            nc.scalar.activation(r, sums[(0, e, half)][:].rearrange("p t (k n) -> p k n t", k=PACK), RELU)
            relus[(e, half)] = r

        def hide(e, half):
            h = work.tile([P, HALF, PACK], BF16, name="h", align_bytes=64)
            nc.vector.tensor_tensor(
                h[:].rearrange("p (k n) t -> p k n t", k=PACK),
                sums[(1, e, half)][:].rearrange("p t (k n) -> p k n t", k=PACK),
                relus[(e, half)],
                MULT,
            )
            hidden[(e, half)] = h

        def quantise_h(e, half):
            words = work.tile([P, HALF], U32, name="h_words", align_bytes=64)
            scales = work.tile([P, HALF], U8, name="h_scales", align_bytes=64)
            nc.vector.quantize_mx(
                out=words[:].bitcast(FP8X4),
                scales=scales[:],
                in_=hidden[(e, half)][:].rearrange("p n t -> p (n t)"),
            )
            hidden_q[(e, half)] = (words, scales)

        def project_back(e, half):
            acc = psum_y.tile([P, HALF], F32, name="acc_y")
            w_words, w_scales = w2_quantised[e]
            h_words, h_scales = hidden_q[(e, half)]
            nc.tensor.matmul_mx(
                out=acc[:],
                lhsT=w_words[:].bitcast(FP8X4),
                lhsT_scale=w_scales[:],
                rhs=h_words[:].bitcast(FP8X4),
                rhs_scale=h_scales[:],
                start=True,
                stop=True,
            )
            results[(e, half)] = acc

        def keep_y(e, half):
            a = e * C + half * HALF
            copy = nc.scalar.copy if e == E - 1 else nc.vector.tensor_copy
            copy(y_all[:, a : a + HALF], results[(e, half)][:])

        def load_next(i):
            if i < len(tiles):
                load(i)
                if i % 4 == 3:
                    load_w2(i // 4)

        for i in range(AHEAD):
            load_next(i)
        for s in range(PASSES):
            dst = x_bf[s][:].rearrange("p (c i t) -> p c t i", i=4, t=PACK)
            src = x_raw[s][:].rearrange("p t (c i) -> p c t i", i=4)
            nc.scalar.copy(dst[:, 128:192], src[:, 128:192])
            nc.vector.tensor_copy(dst[:, 0:128], src[:, 0:128])
            for a, b in ((0, 512), (512, 768)):
                nc.vector.quantize_mx(
                    out=x_words[s][:, a:b].bitcast(FP8X4),
                    scales=x_bytes[SCALE_ROW[s] : P, a:b],
                    in_=x_bf[s][:, PACK * a : PACK * b],
                )
            gather_words(0, s)
        gather_bytes(0)
        nc.sync.dma_start(pos1_t[:], pos1)
        nc.sync.dma_start(pos2_t[:], pos2)

        gate_t = None
        for i in range(len(tiles) + 4):
            e, r = divmod(i, 4)
            load_next(i + AHEAD)
            if i + AHEAD == last:
                gate_t = stage.tile([P, 2, T], F32, name="raw")
                nc.sync.dma_start(out=gate_t[:], in_=gate.rearrange("r p t -> p r t"))
            if i <= last:
                cast_w(i, LAST_SHARE if i == last else SHARE)
            if 1 <= i <= last + 1:
                quantise_w(i - 1)
            if r == 2 and e < E:
                for half in range(2):
                    project(0, e, half)
            if r == 3 and e < E:
                cast_w2(e)
                for half in range(2):
                    rectify(e, half)
            if r == 0 and e > 0:
                for half in range(2):
                    project(1, e - 1, half)
                quantise_w2(e - 1)
            if r == 1 and e > 0:
                for half in range(2):
                    hide(e - 1, half)
            if r == 2 and e > 0:
                for half in range(2):
                    quantise_h(e - 1, half)
                for half in range(2):
                    project_back(e - 1, half)
            if r == 3 and e > 0:
                for half in range(2):
                    keep_y(e - 1, half)
            if i in (6, 7):
                gather_words(1, i - 6)
            if i == 8:
                gather_bytes(1)
            if i in (12, 13):
                gather_words(2, i - 12)
            if i == 14:
                gather_bytes(2)

        pieces = ((0, 512), (512, T))
        products = {}

        def fetch(piece, which, pos_t):
            a, b = piece
            prod = work.tile([P, b - a], F32, name=f"prod{which}", bufs=2)
            nc.vector.tensor_tensor(
                prod[:], y_all[:].indirect(pos_t[:, a // 16 : b // 16]), gate_t[:, which, a:b], MULT
            )
            products[(piece, which)] = prod

        def finish(piece):
            a, b = piece
            o = work.tile([P, b - a], F32, name="o", bufs=2)
            nc.vector.tensor_tensor(o[:], products[(piece, 0)][:], products[(piece, 1)][:], ADD)
            nc.sync.dma_start(out=out[:, a:b], in_=o[:])

        fetch(pieces[0], 0, pos1_t)
        fetch(pieces[0], 1, pos2_t)
        fetch(pieces[1], 0, pos1_t)
        fetch(pieces[1], 1, pos2_t)
        finish(pieces[0])
        finish(pieces[1])
